import numpy as np
CORES = [5,13,21,29,37,45,53,61,69,77,85,93,101,109,117,125]
N = 16
PERM = [[0,9],[1,4],[2,14],[3,7],[4,0],[5,11],[6,3],[7,12],[8,1],[9,15],[10,6],[11,2],[12,10],[13,8],[14,13],[15,5]]
def setup_inputs(rng):
    return {"x": rng.standard_normal((N, 128, 4096), dtype=np.float32)}
def reference(x):
    y = np.empty_like(x)
    for s, d in PERM:
        y[d] = x[s]
    return {"y": y}

@@ -1,0 +1,87 @@
+from concourse.bass import DstId, RemoteDMATransfer
+
+ROUNDS = 4
+ROWS = 128 // (4 * ROUNDS)
+W = 32 * ROWS
+
+SCRATCH = {
+    "stage": ("dram", [4 * ROUNDS, 128, W], "float32"),
+    "land": ("dram", [4 * ROUNDS, 128, W], "float32"),
+}
+SEMAPHORES = ["ld0", "ld1", "ld2", "ld3", "a0", "a1", "a2", "a3", "st", "sent"]
+
+OFF = 0x00FF
+QUART = (0x000F, 0x00F0, 0x0F00, 0xF000)
+
+
+def rank_program(g, core, T, topo):
+    chip, k = topo.chip(core), core % 8
+    rank_at = {topo.chip(c): r for r, c in enumerate(T.cores)}
+    dst_of = {s: d for s, d in T.tables["PERM"]}
+    src_of = {d: s for s, d in T.tables["PERM"]}
+    arr = [T.sem.a0, T.sem.a1, T.sem.a2, T.sem.a3]
+    ld = [T.sem.ld0, T.sem.ld1, T.sem.ld2, T.sem.ld3]
+
+    def on(ch, kk):
+        return ch * 8 + kk
+
+    def forward(q, dst, need):
+        a = topo.addr(dst)
+        for r in range(ROUNDS):
+            g.wait_ge(arr[r], need)
+            g.remote_dma(T.land[4 * r + q], T.land[4 * r + q], arr[r], T.sem.sent, a[1], a[0], OFF)
+        g.wait_ge(T.sem.sent, 8 * ROUNDS)
+
+    if k in (1, 6, 2):
+        s = rank_at[chip]
+        dcore = T.cores[dst_of[s]]
+        dchip = topo.chip(dcore)
+        same = (chip & 1) == (dchip & 1)
+        if k == 1:
+            forward(1, dcore if same else on(dchip ^ 1, 3), 4)
+        elif k == 6:
+            forward(2, on(dchip ^ 1, 7) if same else dcore, 4)
+        else:
+            forward(3, on(dchip ^ 1, 3) if same else dcore, 4)
+        return
+    if k in (7, 3):
+        d = rank_at[chip ^ 1]
+        schip = topo.chip(T.cores[src_of[d]])
+        same = (schip & 1) == ((chip ^ 1) & 1)
+        if k == 7:
+            forward(2 if same else 0, T.cores[d], 8 if same else 4)
+        else:
+            forward(3 if same else 1, T.cores[d], 8)
+        return
+    if k != 5:
+        return
+
+    me = T.rank_of(core)
+    dcore = T.cores[dst_of[me]]
+    dchip = topo.chip(dcore)
+    same = (chip & 1) == (dchip & 1)
+    targets = (dcore if same else on(dchip ^ 1, 7), on(chip, 1), on(chip, 6), on(chip, 2))
+    ids = [DstId(rid=topo.addr(t)[0], pnc=topo.addr(t)[1]) for t in targets]
+
+    def load(r):
+        g.dma_start(T.stage[4 * r:4 * r + 4], T.x[4 * ROWS * r:4 * ROWS * (r + 1), :]).then_inc(ld[r], 16)
+
+    load(0)
+    if ROUNDS > 1:
+        load(1)
+    for r in range(ROUNDS):
+        g.wait_ge(ld[r], 16)
+        g.remote_dma_fused(
+            [RemoteDMATransfer(dst_ids=[ids[q]], dma_engine_mask=QUART[q], remote_sem=arr[r],
+                               src=T.stage[4 * r + q], dst=T.land[4 * r + q]) for q in range(4)],
+            local_sem=T.sem.sent)
+        if r + 2 < ROUNDS:
+            load(r + 2)
+
+    ssame = (topo.chip(T.cores[src_of[me]]) & 1) == (chip & 1)
+    need = 4 + 8 + 8 + 8 if ssame else 32
+    for r in range(ROUNDS):
+        g.wait_ge(arr[r], need)
+        g.dma_start(T.y[4 * ROWS * r:4 * ROWS * (r + 1), :], T.land[4 * r:4 * r + 4]).then_inc(T.sem.st, 16)
+    g.wait_ge(T.sem.st, 16 * ROUNDS)
+    g.wait_ge(T.sem.sent, 16 * ROUNDS)

@@ -1,87 +1,105 @@
 from concourse.bass import DstId, RemoteDMATransfer
 
-ROUNDS = 4
-ROWS = 128 // (4 * ROUNDS)
-W = 32 * ROWS
+STREAMS = 4
+SIZES = [8, 8, 8, 8]
+ROUNDS = len(SIZES)
+AHEAD = 2
+assert STREAMS * sum(SIZES) == 128
 
-SCRATCH = {
-    "stage": ("dram", [4 * ROUNDS, 128, W], "float32"),
-    "land": ("dram", [4 * ROUNDS, 128, W], "float32"),
-}
-SEMAPHORES = ["ld0", "ld1", "ld2", "ld3", "a0", "a1", "a2", "a3", "st", "sent"]
+SCRATCH = {}
+for i in range(8):
+    w = 32 * (SIZES[i] if i < ROUNDS else 1)
+    SCRATCH["stage%d" % i] = ("dram", [STREAMS, 128, w], "float32")
+    SCRATCH["land%d" % i] = ("dram", [STREAMS, 128, w], "float32")
+SEMAPHORES = ["ld%d" % i for i in range(8)] + ["a%d" % i for i in range(32)] + ["st", "sent"]
 
-OFF = 0x00FF
-QUART = (0x000F, 0x00F0, 0x0F00, 0xF000)
+
+def ways(s, d):
+    m = d ^ 1
+    if (s & 1) == (d & 1):
+        return [[s * 8 + 4], [s * 8 + 1], [s * 8 + 6, m * 8 + 7], [s * 8 + 2, m * 8 + 3]]
+    return [[s * 8 + 4, m * 8 + 7], [s * 8 + 1, m * 8 + 3], [s * 8 + 6], [s * 8 + 2]]
+
+
+def plan(T, topo):
+    out = {}
+    for s, d in T.tables["PERM"]:
+        cs, cd = T.cores[s], T.cores[d]
+        for q, mids in enumerate(ways(topo.chip(cs), topo.chip(cd))):
+            path = [cs] + mids + [cd]
+            for i in range(len(path) - 1):
+                out.setdefault(path[i], []).append([q, path[i - 1] if i else None, path[i + 1]])
+    hops = {}
+    for c, lst in out.items():
+        lst.sort(key=lambda h: (topo.chip(h[2]) == topo.chip(c), h[0]))
+        width = 16 if all(topo.chip(h[2]) == topo.chip(c) for h in lst) else 8
+        if len(lst) == STREAMS and c in T.cores:
+            width = 16
+        per = 1
+        while per * 2 * len(lst) <= width:
+            per *= 2
+        hops[c] = [(h[0], h[1], h[2], ((1 << per) - 1) << (per * i), per) for i, h in enumerate(lst)]
+        for h in hops[c]:
+            assert topo.may_write(c, h[2]) and (h[3] & ~topo.mask(c, h[2])) == 0
+    return hops
 
 
 def rank_program(g, core, T, topo):
-    chip, k = topo.chip(core), core % 8
-    rank_at = {topo.chip(c): r for r, c in enumerate(T.cores)}
-    dst_of = {s: d for s, d in T.tables["PERM"]}
-    src_of = {d: s for s, d in T.tables["PERM"]}
-    arr = [T.sem.a0, T.sem.a1, T.sem.a2, T.sem.a3]
-    ld = [T.sem.ld0, T.sem.ld1, T.sem.ld2, T.sem.ld3]
+    hops = plan(T, topo)
+    if core not in hops:
+        return
+    arr = [T.sem.a0, T.sem.a1, T.sem.a2, T.sem.a3, T.sem.a4, T.sem.a5, T.sem.a6, T.sem.a7,
+           T.sem.a8, T.sem.a9, T.sem.a10, T.sem.a11, T.sem.a12, T.sem.a13, T.sem.a14, T.sem.a15,
+           T.sem.a16, T.sem.a17, T.sem.a18, T.sem.a19, T.sem.a20, T.sem.a21, T.sem.a22, T.sem.a23,
+           T.sem.a24, T.sem.a25, T.sem.a26, T.sem.a27, T.sem.a28, T.sem.a29, T.sem.a30, T.sem.a31]
+    ld = [T.sem.ld0, T.sem.ld1, T.sem.ld2, T.sem.ld3, T.sem.ld4, T.sem.ld5, T.sem.ld6, T.sem.ld7]
+    stage = [T.stage0, T.stage1, T.stage2, T.stage3, T.stage4, T.stage5, T.stage6, T.stage7]
+    land = [T.land0, T.land1, T.land2, T.land3, T.land4, T.land5, T.land6, T.land7]
+    mine = hops[core]
 
-    def on(ch, kk):
-        return ch * 8 + kk
+    def engines_into(c, q, prev):
+        return [h[4] for h in hops[prev] if h[0] == q and h[2] == c][0]
 
-    def forward(q, dst, need):
-        a = topo.addr(dst)
+    def send(r, group, src):
+        g.remote_dma_fused(
+            [RemoteDMATransfer(dst_ids=[DstId(rid=topo.addr(h[2])[0], pnc=topo.addr(h[2])[1])],
+                               dma_engine_mask=h[3], remote_sem=arr[r * STREAMS + h[0]],
+                               src=src[r][h[0]], dst=land[r][h[0]]) for h in group],
+            local_sem=T.sem.sent)
+
+    if T.rank_of(core) is None:
+        assert len({h[0] for h in mine}) == len(mine)
+        prevs = sorted({h[1] for h in mine})
         for r in range(ROUNDS):
-            g.wait_ge(arr[r], need)
-            g.remote_dma(T.land[4 * r + q], T.land[4 * r + q], arr[r], T.sem.sent, a[1], a[0], OFF)
-        g.wait_ge(T.sem.sent, 8 * ROUNDS)
-
-    if k in (1, 6, 2):
-        s = rank_at[chip]
-        dcore = T.cores[dst_of[s]]
-        dchip = topo.chip(dcore)
-        same = (chip & 1) == (dchip & 1)
-        if k == 1:
-            forward(1, dcore if same else on(dchip ^ 1, 3), 4)
-        elif k == 6:
-            forward(2, on(dchip ^ 1, 7) if same else dcore, 4)
-        else:
-            forward(3, on(dchip ^ 1, 3) if same else dcore, 4)
-        return
-    if k in (7, 3):
-        d = rank_at[chip ^ 1]
-        schip = topo.chip(T.cores[src_of[d]])
-        same = (schip & 1) == ((chip ^ 1) & 1)
-        if k == 7:
-            forward(2 if same else 0, T.cores[d], 8 if same else 4)
-        else:
-            forward(3 if same else 1, T.cores[d], 8)
-        return
-    if k != 5:
+            for p in prevs:
+                group = [h for h in mine if h[1] == p]
+                for h in group:
+                    g.wait_ge(arr[r * STREAMS + h[0]], engines_into(core, h[0], p))
+                send(r, group, land)
+        g.wait_ge(T.sem.sent, ROUNDS * sum(h[4] for h in mine))
         return
 
-    me = T.rank_of(core)
-    dcore = T.cores[dst_of[me]]
-    dchip = topo.chip(dcore)
-    same = (chip & 1) == (dchip & 1)
-    targets = (dcore if same else on(dchip ^ 1, 7), on(chip, 1), on(chip, 6), on(chip, 2))
-    ids = [DstId(rid=topo.addr(t)[0], pnc=topo.addr(t)[1]) for t in targets]
+    row0 = [STREAMS * sum(SIZES[:r]) for r in range(ROUNDS + 1)]
 
     def load(r):
-        g.dma_start(T.stage[4 * r:4 * r + 4], T.x[4 * ROWS * r:4 * ROWS * (r + 1), :]).then_inc(ld[r], 16)
+        g.dma_start(stage[r][:], T.x[row0[r]:row0[r + 1], :]).then_inc(ld[r], 16)
 
-    load(0)
-    if ROUNDS > 1:
-        load(1)
+    for r in range(min(AHEAD, ROUNDS)):
+        load(r)
     for r in range(ROUNDS):
         g.wait_ge(ld[r], 16)
-        g.remote_dma_fused(
-            [RemoteDMATransfer(dst_ids=[ids[q]], dma_engine_mask=QUART[q], remote_sem=arr[r],
-                               src=T.stage[4 * r + q], dst=T.land[4 * r + q]) for q in range(4)],
-            local_sem=T.sem.sent)
-        if r + 2 < ROUNDS:
-            load(r + 2)
+        send(r, mine, stage)
+        if r + AHEAD < ROUNDS:
+            load(r + AHEAD)
 
-    ssame = (topo.chip(T.cores[src_of[me]]) & 1) == (chip & 1)
-    need = 4 + 8 + 8 + 8 if ssame else 32
+    last = {}
+    for c, lst in hops.items():
+        for h in lst:
+            if h[2] == core:
+                last[h[0]] = h[4]
     for r in range(ROUNDS):
-        g.wait_ge(arr[r], need)
-        g.dma_start(T.y[4 * ROWS * r:4 * ROWS * (r + 1), :], T.land[4 * r:4 * r + 4]).then_inc(T.sem.st, 16)
+        for q in range(STREAMS):
+            g.wait_ge(arr[r * STREAMS + q], last[q])
+        g.dma_start(T.y[row0[r]:row0[r + 1], :], land[r][:]).then_inc(T.sem.st, 16)
     g.wait_ge(T.sem.st, 16 * ROUNDS)
-    g.wait_ge(T.sem.sent, 16 * ROUNDS)
+    g.wait_ge(T.sem.sent, ROUNDS * sum(h[4] for h in mine))

@@ -1,23 +1,23 @@
 from concourse.bass import DstId, RemoteDMATransfer
 
-STREAMS = 4
-SIZES = [8, 8, 8, 8]
+SIZES = [4, 6, 6, 6, 6, 4]
 ROUNDS = len(SIZES)
-AHEAD = 2
-assert STREAMS * sum(SIZES) == 128
+LANES = [[0, 1, 2, 3]] * ROUNDS
+AHEAD = 3
+assert 4 * sum(SIZES) == 128
 
 SCRATCH = {}
 for i in range(8):
     w = 32 * (SIZES[i] if i < ROUNDS else 1)
-    SCRATCH["stage%d" % i] = ("dram", [STREAMS, 128, w], "float32")
-    SCRATCH["land%d" % i] = ("dram", [STREAMS, 128, w], "float32")
+    SCRATCH["stage%d" % i] = ("dram", [4, 128, w], "float32")
+    SCRATCH["land%d" % i] = ("dram", [4, 128, w], "float32")
 SEMAPHORES = ["ld%d" % i for i in range(8)] + ["a%d" % i for i in range(32)] + ["st", "sent"]
 
 
 def ways(s, d):
     m = d ^ 1
     if (s & 1) == (d & 1):
-        return [[s * 8 + 4], [s * 8 + 1], [s * 8 + 6, m * 8 + 7], [s * 8 + 2, m * 8 + 3]]
+        return [[s * 8 + 6, m * 8 + 7], [s * 8 + 2, m * 8 + 3], [s * 8 + 4], [s * 8 + 1]]
     return [[s * 8 + 4, m * 8 + 7], [s * 8 + 1, m * 8 + 3], [s * 8 + 6], [s * 8 + 2]]
 
 
@@ -25,28 +25,25 @@ def plan(T, topo):
     out = {}
     for s, d in T.tables["PERM"]:
         cs, cd = T.cores[s], T.cores[d]
-        for q, mids in enumerate(ways(topo.chip(cs), topo.chip(cd))):
-            path = [cs] + mids + [cd]
-            for i in range(len(path) - 1):
-                out.setdefault(path[i], []).append([q, path[i - 1] if i else None, path[i + 1]])
-    hops = {}
-    for c, lst in out.items():
-        lst.sort(key=lambda h: (topo.chip(h[2]) == topo.chip(c), h[0]))
-        width = 16 if all(topo.chip(h[2]) == topo.chip(c) for h in lst) else 8
-        if len(lst) == STREAMS and c in T.cores:
-            width = 16
-        per = 1
-        while per * 2 * len(lst) <= width:
-            per *= 2
-        hops[c] = [(h[0], h[1], h[2], ((1 << per) - 1) << (per * i), per) for i, h in enumerate(lst)]
-        for h in hops[c]:
-            assert topo.may_write(c, h[2]) and (h[3] & ~topo.mask(c, h[2])) == 0
-    return hops
+        w = ways(topo.chip(cs), topo.chip(cd))
+        for r in range(ROUNDS):
+            for j in range(4):
+                path = [cs] + w[LANES[r][j]] + [cd]
+                for i in range(len(path) - 1):
+                    out.setdefault((path[i], r), []).append((j, path[i + 1]))
+    hops, into = {}, {}
+    for (c, r), lst in out.items():
+        per = (16 if c in T.cores else 8) // len(lst)
+        hops[c, r] = [(j, nx, ((1 << per) - 1) << (per * i), per) for i, (j, nx) in enumerate(lst)]
+        for j, nx, mask, per in hops[c, r]:
+            assert topo.may_write(c, nx) and (mask & ~topo.mask(c, nx)) == 0 and (nx, r, j) not in into
+            into[nx, r, j] = per
+    return hops, into
 
 
 def rank_program(g, core, T, topo):
-    hops = plan(T, topo)
-    if core not in hops:
+    hops, into = plan(T, topo)
+    if not any((core, r) in hops for r in range(ROUNDS)):
         return
     arr = [T.sem.a0, T.sem.a1, T.sem.a2, T.sem.a3, T.sem.a4, T.sem.a5, T.sem.a6, T.sem.a7,
            T.sem.a8, T.sem.a9, T.sem.a10, T.sem.a11, T.sem.a12, T.sem.a13, T.sem.a14, T.sem.a15,
@@ -55,31 +52,25 @@ def rank_program(g, core, T, topo):
     ld = [T.sem.ld0, T.sem.ld1, T.sem.ld2, T.sem.ld3, T.sem.ld4, T.sem.ld5, T.sem.ld6, T.sem.ld7]
     stage = [T.stage0, T.stage1, T.stage2, T.stage3, T.stage4, T.stage5, T.stage6, T.stage7]
     land = [T.land0, T.land1, T.land2, T.land3, T.land4, T.land5, T.land6, T.land7]
-    mine = hops[core]
+    left = sum(h[3] for r in range(ROUNDS) for h in hops.get((core, r), []))
 
-    def engines_into(c, q, prev):
-        return [h[4] for h in hops[prev] if h[0] == q and h[2] == c][0]
-
-    def send(r, group, src):
+    def send(r, src):
         g.remote_dma_fused(
-            [RemoteDMATransfer(dst_ids=[DstId(rid=topo.addr(h[2])[0], pnc=topo.addr(h[2])[1])],
-                               dma_engine_mask=h[3], remote_sem=arr[r * STREAMS + h[0]],
-                               src=src[r][h[0]], dst=land[r][h[0]]) for h in group],
+            [RemoteDMATransfer(dst_ids=[DstId(rid=topo.addr(nx)[0], pnc=topo.addr(nx)[1])],
+                               dma_engine_mask=mask, remote_sem=arr[r * 4 + j],
+                               src=src[r][j], dst=land[r][j]) for j, nx, mask, per in hops[core, r]],
             local_sem=T.sem.sent)
 
     if T.rank_of(core) is None:
-        assert len({h[0] for h in mine}) == len(mine)
-        prevs = sorted({h[1] for h in mine})
         for r in range(ROUNDS):
-            for p in prevs:
-                group = [h for h in mine if h[1] == p]
-                for h in group:
-                    g.wait_ge(arr[r * STREAMS + h[0]], engines_into(core, h[0], p))
-                send(r, group, land)
-        g.wait_ge(T.sem.sent, ROUNDS * sum(h[4] for h in mine))
+            if (core, r) in hops:
+                for h in hops[core, r]:
+                    g.wait_ge(arr[r * 4 + h[0]], into[core, r, h[0]])
+                send(r, land)
+        g.wait_ge(T.sem.sent, left)
         return
 
-    row0 = [STREAMS * sum(SIZES[:r]) for r in range(ROUNDS + 1)]
+    row0 = [4 * sum(SIZES[:r]) for r in range(ROUNDS + 1)]
 
     def load(r):
         g.dma_start(stage[r][:], T.x[row0[r]:row0[r + 1], :]).then_inc(ld[r], 16)
@@ -88,18 +79,13 @@ def rank_program(g, core, T, topo):
         load(r)
     for r in range(ROUNDS):
         g.wait_ge(ld[r], 16)
-        send(r, mine, stage)
+        send(r, stage)
         if r + AHEAD < ROUNDS:
             load(r + AHEAD)
 
-    last = {}
-    for c, lst in hops.items():
-        for h in lst:
-            if h[2] == core:
-                last[h[0]] = h[4]
     for r in range(ROUNDS):
-        for q in range(STREAMS):
-            g.wait_ge(arr[r * STREAMS + q], last[q])
+        for j in range(4):
+            g.wait_ge(arr[r * 4 + j], into[core, r, j])
         g.dma_start(T.y[row0[r]:row0[r + 1], :], land[r][:]).then_inc(T.sem.st, 16)
     g.wait_ge(T.sem.st, 16 * ROUNDS)
-    g.wait_ge(T.sem.sent, ROUNDS * sum(h[4] for h in mine))
+    g.wait_ge(T.sem.sent, left)

from concourse.bass import DstId, RemoteDMATransfer

SIZES = [4, 6, 6, 6, 6, 4]
ROUNDS = len(SIZES)
LANES = [[0, 1, 2, 3]] * ROUNDS
AHEAD = 3
assert 4 * sum(SIZES) == 128

SCRATCH = {}
for i in range(8):
    w = 32 * (SIZES[i] if i < ROUNDS else 1)
    SCRATCH["stage%d" % i] = ("dram", [4, 128, w], "float32")
    SCRATCH["land%d" % i] = ("dram", [4, 128, w], "float32")
SEMAPHORES = ["ld%d" % i for i in range(8)] + ["a%d" % i for i in range(32)] + ["st", "sent"]


def ways(s, d):
    m = d ^ 1
    if (s & 1) == (d & 1):
        return [[s * 8 + 6, m * 8 + 7], [s * 8 + 2, m * 8 + 3], [s * 8 + 4], [s * 8 + 1]]
    return [[s * 8 + 4, m * 8 + 7], [s * 8 + 1, m * 8 + 3], [s * 8 + 6], [s * 8 + 2]]


def plan(T, topo):
    out = {}
    for s, d in T.tables["PERM"]:
        cs, cd = T.cores[s], T.cores[d]
        w = ways(topo.chip(cs), topo.chip(cd))
        for r in range(ROUNDS):
            for j in range(4):
                path = [cs] + w[LANES[r][j]] + [cd]
                for i in range(len(path) - 1):
                    out.setdefault((path[i], r), []).append((j, path[i + 1]))
    hops, into = {}, {}
    for (c, r), lst in out.items():
        per = (16 if c in T.cores else 8) // len(lst)
        hops[c, r] = [(j, nx, ((1 << per) - 1) << (per * i), per) for i, (j, nx) in enumerate(lst)]
        for j, nx, mask, per in hops[c, r]:
            assert topo.may_write(c, nx) and (mask & ~topo.mask(c, nx)) == 0 and (nx, r, j) not in into
            into[nx, r, j] = per
    return hops, into


def rank_program(g, core, T, topo):
    hops, into = plan(T, topo)
    if not any((core, r) in hops for r in range(ROUNDS)):
        return
    arr = [T.sem.a0, T.sem.a1, T.sem.a2, T.sem.a3, T.sem.a4, T.sem.a5, T.sem.a6, T.sem.a7,
           T.sem.a8, T.sem.a9, T.sem.a10, T.sem.a11, T.sem.a12, T.sem.a13, T.sem.a14, T.sem.a15,
           T.sem.a16, T.sem.a17, T.sem.a18, T.sem.a19, T.sem.a20, T.sem.a21, T.sem.a22, T.sem.a23,
           T.sem.a24, T.sem.a25, T.sem.a26, T.sem.a27, T.sem.a28, T.sem.a29, T.sem.a30, T.sem.a31]
    ld = [T.sem.ld0, T.sem.ld1, T.sem.ld2, T.sem.ld3, T.sem.ld4, T.sem.ld5, T.sem.ld6, T.sem.ld7]
    stage = [T.stage0, T.stage1, T.stage2, T.stage3, T.stage4, T.stage5, T.stage6, T.stage7]
    land = [T.land0, T.land1, T.land2, T.land3, T.land4, T.land5, T.land6, T.land7]
    left = sum(h[3] for r in range(ROUNDS) for h in hops.get((core, r), []))

    def send(r, src):
        g.remote_dma_fused(
            [RemoteDMATransfer(dst_ids=[DstId(rid=topo.addr(nx)[0], pnc=topo.addr(nx)[1])],
                               dma_engine_mask=mask, remote_sem=arr[r * 4 + j],
                               src=src[r][j], dst=land[r][j]) for j, nx, mask, per in hops[core, r]],
            local_sem=T.sem.sent)

    if T.rank_of(core) is None:
        for r in range(ROUNDS):
            if (core, r) in hops:
                for h in hops[core, r]:
                    g.wait_ge(arr[r * 4 + h[0]], into[core, r, h[0]])
                send(r, land)
        g.wait_ge(T.sem.sent, left)
        return

    row0 = [4 * sum(SIZES[:r]) for r in range(ROUNDS + 1)]

    def load(r):
        g.dma_start(stage[r][:], T.x[row0[r]:row0[r + 1], :]).then_inc(ld[r], 16)

    for r in range(min(AHEAD, ROUNDS)):
        load(r)
    for r in range(ROUNDS):
        g.wait_ge(ld[r], 16)
        send(r, stage)
        if r + AHEAD < ROUNDS:
            load(r + AHEAD)

    for r in range(ROUNDS):
        for j in range(4):
            g.wait_ge(arr[r * 4 + j], into[core, r, j])
        g.dma_start(T.y[row0[r]:row0[r + 1], :], land[r][:]).then_inc(T.sem.st, 16)
    g.wait_ge(T.sem.st, 16 * ROUNDS)
    g.wait_ge(T.sem.sent, left)
